import numpy as np, ml_dtypes
CORES = [61,69,101,62,70,102]
N = 6
import mx_ref
NC, G = 256, 4
C = np.float32(0.043)
WID = [224,160,128,128,256,128]
BF = ml_dtypes.bfloat16
def cut(t, i, w=512):
    return t[:, w * i:w * i + w]
def tile(rs):
    return np.stack(rs, axis=2).reshape(128, -1).astype(BF)
def layer(w, X):
    out = []
    for i in range(G):
        for t in range(len(X)):
            p = mx_ref.matmul(mx_ref.quantize(cut(w, len(X) * i + t)), X[t])
            z = p if t == 0 else z + p
        out.append(z)
    return out
def act(Z):
    return [np.maximum(z, 0) * C for z in Z]
def setup_inputs(rng):
    def f(*shape):
        return mx_ref.flush((rng.standard_normal(shape, dtype=np.float32) * np.exp2(rng.integers(-2, 3, shape[:-1] + (1,)))).astype(BF))
    return {"x": f(N, 128, 4 * NC), "w1": f(N, 128, G * 512), "w2": f(N, 128, 512)}
def setup_inputs_blocks(rng):
    d = setup_inputs(rng)
    for k in ("x", "w1", "w2"): d[k] = mx_ref.spread(d[k], rng, 2)
    return d
def setup_inputs_wide(rng):
    d = setup_inputs(rng)
    for k in ("x", "w1", "w2"): d[k] = mx_ref.flush((d[k].astype(np.float32) * np.exp2(rng.integers(-6, 7, (N, 1, 1))).astype(np.float32)).astype(BF))
    return d
def reference(x, w1, w2):
    X = [mx_ref.quantize(x[j][:, :4 * WID[j]]) for j in range(N)]
    y = np.full((N, 128, NC), np.nan, np.float32)
    for c in range(N):
        for r in range(N):
            p = mx_ref.matmul(mx_ref.quantize(w2[r]), mx_ref.quantize(tile(act(layer(w1[r], [X[c]])))))
            z = p if r == 0 else z + p
        y[c][:, :WID[c]] = z
    return {"y": y}

@@ -1,0 +1,380 @@
+import numpy as np
+from concourse.bass import DstId, RemoteDMATransfer
+from concourse.mybir import dt, AluOpType, ActivationFunctionType
+
+C = float(np.float32(0.043))
+LAY = {
+    0: [(0, 0, 224), (3, 0, 128), (4, 0, 224)],
+    3: [(3, 0, 128), (4, 224, 256), (5, 0, 128), (1, 0, 160), (2, 0, 128)],
+    1: [(1, 0, 160), (4, 0, 96), (2, 0, 128), (5, 0, 128)],
+    4: [(4, 0, 256), (3, 0, 128), (0, 0, 224)],
+    2: [(2, 0, 128), (1, 0, 160), (4, 0, 224)],
+    5: [(5, 0, 128), (4, 224, 256), (3, 0, 128), (0, 0, 224)],
+}
+TILES = {
+    0: [(0, 0, 224, 0), (0, 224, 128, 0), (0, 352, 224, 0), (3, 352, 224, 0), (3, 0, 224, 2)],
+    3: [(3, 0, 128, 0), (3, 128, 160, 0), (0, 128, 160, 0), (3, 288, 160, 0), (0, 288, 160, 2), (3, 448, 128, 0), (0, 448, 128, 2)],
+    1: [(1, 0, 128, 0), (1, 128, 128, 0), (1, 256, 128, 0), (1, 384, 128, 0),
+        (4, 256, 128, 0), (4, 384, 128, 2), (4, 128, 128, 2), (4, 0, 128, 2)],
+    4: [(4, 96, 160, 0), (4, 256, 128, 0), (1, 256, 128, 0), (4, 384, 224, 0), (1, 384, 224, 2), (1, 96, 160, 2)],
+    2: [(2, 0, 128, 0), (2, 128, 160, 0), (2, 288, 224, 0), (5, 128, 160, 0), (5, 288, 224, 2), (5, 0, 128, 2)],
+    5: [(5, 0, 128, 0), (5, 128, 160, 0), (2, 128, 160, 0), (5, 288, 224, 0), (2, 288, 224, 2), (2, 0, 128, 2)],
+}
+XSEND = {
+    0: [[(0, 224, [4, 5], "all")]],
+    3: [[(0, 128, [4, 5], "lo"), (0, 128, [0], "hi")]],
+    1: [[(0, 160, [2], "lo"), (0, 160, [3], "hi")]],
+    4: [[(0, 224, [0, 2], "lo")], [(224, 256, [3, 5], "lo")], [(0, 96, [1], "hi")]],
+    2: [[(0, 128, [1], "lo"), (0, 128, [3], "hi")]],
+    5: [[(0, 128, [1, 3], "lo")]],
+}
+WENG = {0: "all", 1: "all", 2: "all", 3: "hi", 4: "hi", 5: "hi"}
+FIN = {0: [[5], [4]], 3: [[0], [4], [5]], 1: [[2], [3]], 4: [[2, 5], [0, 3]], 2: [[1], [3]], 5: [[1], [3]]}
+
+ZB, YB = 6, 2
+
+SCRATCH = {
+    "xb": ("sbuf", [128, 1024], "bfloat16"),
+    "wb": ("sbuf", [128, 2560], "bfloat16"),
+    "xq": ("sbuf", [128, 640], "float8_e4m3fn_x4"),
+    "xs": ("sbuf", [128, 640], "uint8"),
+    "wq": ("sbuf", [128, 640], "float8_e4m3fn_x4"),
+    "ws": ("sbuf", [128, 640], "uint8"),
+    "pq": ("sbuf", [128, 640], "float8_e4m3fn_x4"),
+    "ps": ("sbuf", [128, 640], "uint8"),
+    "hb": ("sbuf", [128, 4096], "bfloat16"),
+    "hq": ("sbuf", [128, 1024], "float8_e4m3fn_x4"),
+    "hs": ("sbuf", [128, 1024], "uint8"),
+    "z": ("psum", [128, 512 * ZB], "float32"),
+    "yb": ("psum", [128, 512 * YB], "float32"),
+    "own": ("sbuf", [128, 256], "float32"),
+    "l0": ("sbuf", [128, 256], "float32"),
+    "l1": ("sbuf", [128, 256], "float32"),
+    "l2": ("sbuf", [128, 256], "float32"),
+    "yo": ("sbuf", [128, 256], "float32"),
+    "ys": ("sbuf", [128, 512], "float32"),
+}
+SEMAPHORES = (["lx", "lwa", "lwb", "st", "qi", "mm", "ym", "zs", "zv", "hqd", "ev", "fa", "sent",
+               "wpa", "wpb", "hc", "hsc", "hr"]
+              + ["x%d" % i for i in range(6)] + ["r%d" % i for i in range(6)])
+
+
+def _bits(m):
+    return bin(m).count("1")
+
+
+def _masks(topo, cores, core):
+    far = [c for c in cores if topo.chip(c) != topo.chip(core)][0]
+    near = [c for c in cores if topo.chip(c) == topo.chip(core) and c != core][0]
+    lo, al = topo.mask(core, far), topo.mask(core, near)
+    return {"lo": lo, "all": al, "hi": al & ~lo}
+
+
+def _helpers(topo, cores):
+    out = {}
+    for r in range(len(cores)):
+        for c in range(len(cores)):
+            src, dst = cores[r], cores[c]
+            if topo.may_write(src, dst) or not _sends(r, c):
+                continue
+            ch = topo.chip(src)
+            first = src
+            while first > 0 and topo.chip(first - 1) == ch:
+                first -= 1
+            k = first
+            while topo.chip(k) == ch:
+                if k not in cores and k not in out.values() and topo.die(k) != topo.die(src) and topo.may_write(k, dst):
+                    out[(r, c)] = k
+                    break
+                k += 1
+    return out
+
+
+def _sends(r, c):
+    return any(c in t[2] for call in XSEND[r] for t in call)
+
+
+def _xpos(r, c):
+    p = 0
+    for (k, a, b) in LAY[r]:
+        if k == c:
+            return p, a, b
+        p += b - a
+    return None
+
+
+def rank_program(g, core, T, topo):
+    cores = list(T.cores)
+    rank = T.rank_of(core)
+    helpers = _helpers(topo, cores)
+    chips = []
+    for c in cores:
+        if topo.chip(c) not in chips:
+            chips.append(topo.chip(c))
+    if rank is None and core not in helpers.values():
+        return
+    M = _masks(topo, cores, core)
+    S = T.sem
+    seen, top, total = {}, {}, {}
+    Q = {"g": g, "t": g.tensor, "v": g.vector, "s": g.scalar, "y": g.sync}
+
+    def wait(q, name, val):
+        if seen.get((q, name), 0) < val:
+            Q[q].wait_ge(S[name], val)
+            seen[(q, name)] = val
+            top[name] = max(top.get(name, 0), val)
+
+    def inc(name, n=1):
+        total[name] = total.get(name, 0) + n
+        return total[name]
+
+    def did(dst):
+        rid, pid, _ = topo.addr(dst)
+        return DstId(rid=rid, pnc=pid)
+
+    def send(transfers):
+        g.remote_dma_fused([RemoteDMATransfer(dst_ids=[did(d) for d, _ in ds], dma_engine_mask=m, remote_sem=S[sem],
+                                              srcs=[src], dsts=[ap for _, ap in ds], alu_op=0)
+                            for (src, ds, m, sem) in transfers], local_sem=S.sent)
+        for (src, ds, m, sem) in transfers:
+            inc("sent", _bits(m))
+
+    def codes(t, a, b):
+        return t[:, a:b].bitcast(dt.uint8)
+
+    def finish():
+        for name in total:
+            if top.get(name, 0) < total[name]:
+                wait("g", name, total[name])
+
+    if rank is None:
+        for (r, c), h in helpers.items():
+            if h != core:
+                continue
+            n = [(a, b) for call in XSEND[r] for (a, b, ds, e) in call if c in ds][0]
+            e = [e for call in XSEND[r] for (a, b, ds, e) in call if c in ds][0]
+            n = n[1] - n[0]
+            p = _xpos(c, r)[0]
+            cnt = _bits(M[e])
+            wait("g", "hc", cnt)
+            send([(codes(T.xq, 0, n), [(cores[c], codes(T.xq, p, p + n))], M["lo"], "x%d" % r)])
+            wait("g", "hsc", cnt)
+            send([(T.xs[:, 0:n], [(cores[c], T.xs[:, p:p + n])], M["lo"], "x%d" % r)])
+            pos = _xpos(r, c)
+            if pos is not None:
+                _, a, b = pos
+                wait("g", "hr", _bits(M["all"]))
+                lay = T["l%d" % chips.index(topo.chip(core))]
+                send([(T.ys[:, 0:b - a], [(cores[c], lay[:, a:b])], M["lo"], "r%d" % r)])
+        finish()
+        return
+
+    wid = T.tables["WID"][rank]
+    partner = [r for r in range(len(cores)) if r != rank and topo.chip(cores[r]) == topo.chip(core)][0]
+    on_chip = lambda c: topo.chip(cores[c]) == topo.chip(core)
+
+    g.sync.dma_start(T.xb[:, 0:4 * wid], T.x[:, 0:4 * wid]).then_inc(S.lx, 16)
+    g.sync.dma_start(T.wb[:, 0:1024], T.w1[:, 0:1024]).then_inc(S.lwa, 16)
+    g.sync.dma_start(T.wb[:, 1024:2048], T.w1[:, 1024:2048]).then_inc(S.lwb, 16)
+    g.sync.dma_start(T.wb[:, 2048:2560], T.w2[:]).then_inc(S.lwb, 16)
+    inc("lx", 16), inc("lwa", 16), inc("lwb", 32)
+    wait("v", "lx", 16)
+    g.vector.quantize_mx(T.xq[:, 0:wid], T.xs[:, 0:wid], T.xb[:, 0:4 * wid]).then_inc(S.qi, 1)
+    wait("v", "lwa", 16)
+    g.vector.quantize_mx(T.wq[:, 0:256], T.ws[:, 0:256], T.wb[:, 0:1024]).then_inc(S.qi, 1)
+    wait("v", "lwb", 32)
+    g.vector.quantize_mx(T.wq[:, 256:512], T.ws[:, 256:512], T.wb[:, 1024:2048]).then_inc(S.qi, 1)
+    g.vector.quantize_mx(T.wq[:, 512:640], T.ws[:, 512:640], T.wb[:, 2048:2560]).then_inc(S.qi, 1)
+    inc("qi", 4)
+
+    wait("g", "qi", 1)
+    for call in XSEND[rank]:
+        cs, ss = [], []
+        for (a, b, ds, e) in call:
+            relay = [(rank, c) in helpers for c in ds]
+            dc, dp = [], []
+            for c in ds:
+                if (rank, c) in helpers:
+                    h, p = helpers[(rank, c)], 0
+                else:
+                    h, p = cores[c], _xpos(c, rank)[0]
+                dc.append((h, codes(T.xq, p, p + b - a)))
+                dp.append((h, T.xs[:, p:p + b - a]))
+            cs.append((codes(T.xq, a, b), dc, M[e], "hc" if relay[0] else "x%d" % rank))
+            ss.append((T.xs[:, a:b], dp, M[e], "hsc" if relay[0] else "x%d" % rank))
+        send(cs)
+        send(ss)
+    pc = cores[partner]
+    for (a, b, q, sem) in ((0, 256, 2, "wpa"), (256, 640, 4, "wpb")):
+        wait("g", "qi", q)
+        send([(codes(T.wq, a, b), [(pc, codes(T.pq, a, b))], M[WENG[rank]], sem)])
+        send([(T.ws[:, a:b], [(pc, T.ps[:, a:b])], M[WENG[rank]], sem)])
+    wcnt = 2 * _bits(M[WENG[partner]])
+    inc("wpa", wcnt), inc("wpb", wcnt)
+    xcnt = 2 * _bits(M["lo"])
+    for (c, a, b) in LAY[rank][1:]:
+        inc("x%d" % c, xcnt)
+
+    tiles = TILES[rank]
+    groups = {}
+    off = 0
+    toff = []
+    for k, (w, s, n, lag) in enumerate(tiles):
+        groups.setdefault((s, n), []).append(k)
+        toff.append(off)
+        off += n
+
+    mm = 0
+    drain = {}
+    ybank = {}
+    evac_of = []
+    evcount = 0
+    yoff = 0
+    results = []
+    own_ev = 0
+    lagged = None
+    cs_, cv_ = 0, 0
+
+    def second(key):
+        gi = len(ybank)
+        ybank[key] = gi
+        ks = groups[key]
+        n = key[1]
+        if gi >= YB:
+            wait("t", "ev", evac_of[gi - YB])
+        out = T.yb[:, 512 * (gi % YB):512 * (gi % YB) + n]
+        for i, k in enumerate(ks):
+            own_w = tiles[k][0] == rank
+            if own_w:
+                wait("t", "qi", 4)
+            else:
+                wait("t", "wpb", wcnt)
+            wait("t", "hqd", k + 1)
+            W, P = (T.wq, T.ws) if own_w else (T.pq, T.ps)
+            o = toff[k]
+            ins = g.tensor.matmul_mx(out, W[:, 512:640], P[:, 512:640], T.hq[:, o:o + n], T.hs[:, o:o + n],
+                                     i == 0, i == len(ks) - 1)
+            if i == len(ks) - 1:
+                ins.then_inc(S.ym, 1)
+                inc("ym")
+
+    def evacuate(key, state):
+        s, n = key
+        gi = ybank[key]
+        wait("s", "ym", gi + 1)
+        base = 512 * (gi % YB)
+        p = 0
+        runs = []
+        for (c, a, b) in LAY[rank]:
+            lo, hi = max(s, p), min(s + n, p + b - a)
+            if lo < hi:
+                piece = (c, a + lo - p, a + hi - p, lo - s)
+                kind = c == rank
+                if runs and runs[-1][0] == kind:
+                    runs[-1][1].append(piece)
+                else:
+                    runs.append((kind, [piece]))
+            p += b - a
+        for kind, pieces in runs:
+            lo, m = pieces[0][3], sum(q[2] - q[1] for q in pieces)
+            if kind:
+                out = T.own[:, pieces[0][1]:pieces[0][1] + m]
+            else:
+                out = T.ys[:, state["y"]:state["y"] + m]
+            g.scalar.activation(out, T.yb[:, base + lo:base + lo + m], ActivationFunctionType.Copy).then_inc(S.ev, 1)
+            ev = inc("ev")
+            if kind:
+                state["own"] = ev
+            else:
+                for (c, a, b, at) in pieces:
+                    results.append((ev, state["y"] + at - lo, b - a, c, a))
+                state["y"] += m
+        evac_of.append(total["ev"])
+
+    state = {"y": 0, "own": 0}
+    pending = None
+    for k, (w, s, n, lag) in enumerate(tiles):
+        own_w = w == rank
+        W, P = (T.wq, T.ws) if own_w else (T.pq, T.ps)
+        o = 4 * toff[k]
+        for b in range(4):
+            if pending is not None and b == lag:
+                second(pending)
+                evacuate(pending, state)
+                pending = None
+            if b == 0:
+                p = 0
+                for (c, ca, cb) in LAY[rank]:
+                    if max(s, p) < min(s + n, p + cb - ca):
+                        if c == rank:
+                            wait("t", "qi", 1)
+                        else:
+                            wait("t", "x%d" % c, xcnt)
+                    p += cb - ca
+            if own_w:
+                wait("t", "qi", 2 if b < 2 else 3)
+            else:
+                wait("t", "wpa" if b < 2 else "wpb", wcnt)
+            if mm >= ZB:
+                wait("t", *drain[mm - ZB])
+            z = T.z[:, 512 * (mm % ZB):512 * (mm % ZB) + n]
+            g.tensor.matmul_mx(z, W[:, 128 * b:128 * b + 128], P[:, 128 * b:128 * b + 128],
+                               T.xq[:, s:s + n], T.xs[:, s:s + n], True, True).then_inc(S.mm, 1)
+            inc("mm")
+            mm += 1
+            h = T.hb[:, o + b:o + 4 * n:4]
+            if b % 2 == 0:
+                wait("s", "mm", mm)
+                g.scalar.activation(h, z, ActivationFunctionType.Relu, scale=C).then_inc(S.zs, 1)
+                drain[mm - 1] = ("zs", inc("zs"))
+            else:
+                wait("v", "mm", mm)
+                g.vector.tensor_scalar(h, z, 0.0, C, AluOpType.max, AluOpType.mult).then_inc(S.zv, 1)
+                drain[mm - 1] = ("zv", inc("zv"))
+        wait("v", "zs", total["zs"])
+        wait("v", "zv", total["zv"])
+        g.vector.quantize_mx(T.hq[:, toff[k]:toff[k] + n], T.hs[:, toff[k]:toff[k] + n],
+                             T.hb[:, o:o + 4 * n]).then_inc(S.hqd, 1)
+        inc("hqd")
+        if groups[(s, n)][-1] == k:
+            pending = (s, n)
+    second(pending)
+    evacuate(pending, state)
+
+    for (ev, y0, n, c, a) in results:
+        wait("g", "ev", ev)
+        src = T.ys[:, y0:y0 + n]
+        if (rank, c) in helpers:
+            send([(src, [(helpers[(rank, c)], T.ys[:, 0:n])], M["all"], "hr")])
+            continue
+        if on_chip(c) and (len([1 for t in TILES[c] if t[1] <= a < t[1] + t[2]]) == 0):
+            dst, m = T.own[:, a:a + n], M["all"]
+        else:
+            dst, m = T["l%d" % chips.index(topo.chip(core))][:, a:a + n], M["all"] if on_chip(c) else M["lo"]
+        send([(src, [(cores[c], dst)], m, "r%d" % rank)])
+
+    rcnt = {}
+    for r in range(len(cores)):
+        if r != rank and _xpos(r, rank) is not None:
+            rcnt[r] = _bits(M["all"] if on_chip(r) else M["lo"])
+            inc("r%d" % r, rcnt[r])
+    wait("v", "ev", state["own"])
+    layers = FIN[rank]
+    for r in rcnt:
+        if on_chip(r) and [r] not in layers:
+            wait("v", "r%d" % r, rcnt[r])
+    acc = T.own
+    for i, senders in enumerate(layers):
+        for r in senders:
+            wait("v", "r%d" % r, rcnt[r])
+        if i:
+            wait("v", "fa", i)
+        lay = T["l%d" % chips.index(topo.chip(cores[senders[0]]))]
+        g.vector.tensor_tensor(T.yo[:, 0:wid], acc[:, 0:wid], lay[:, 0:wid], AluOpType.add).then_inc(S.fa, 1)
+        inc("fa")
+        acc = T.yo
+    wait("y", "fa", len(layers))
+    g.sync.dma_start(T.y[:, 0:wid], T.yo[:, 0:wid]).then_inc(S.st, 16)
+    inc("st", 16)
+    wait("y", "st", 16)
+    finish()

@@ -5,39 +5,50 @@ from concourse.mybir import dt, AluOpType, ActivationFunctionType
 C = float(np.float32(0.043))
 LAY = {
     0: [(0, 0, 224), (3, 0, 128), (4, 0, 224)],
-    3: [(3, 0, 128), (4, 224, 256), (5, 0, 128), (1, 0, 160), (2, 0, 128)],
+    3: [(3, 0, 128), (5, 0, 128), (4, 224, 256), (2, 0, 128), (1, 0, 160)],
     1: [(1, 0, 160), (4, 0, 96), (2, 0, 128), (5, 0, 128)],
-    4: [(4, 0, 256), (3, 0, 128), (0, 0, 224)],
+    4: [(4, 0, 256), (0, 0, 224), (3, 0, 128)],
     2: [(2, 0, 128), (1, 0, 160), (4, 0, 224)],
-    5: [(5, 0, 128), (4, 224, 256), (3, 0, 128), (0, 0, 224)],
+    5: [(5, 0, 128), (4, 224, 256), (0, 0, 224), (3, 0, 128)],
 }
 TILES = {
-    0: [(0, 0, 224, 0), (0, 224, 128, 0), (0, 352, 224, 0), (3, 352, 224, 0), (3, 0, 224, 2)],
-    3: [(3, 0, 128, 0), (3, 128, 160, 0), (0, 128, 160, 0), (3, 288, 160, 0), (0, 288, 160, 2), (3, 448, 128, 0), (0, 448, 128, 2)],
+    0: [(0, 0, 224, 0), (0, 224, 128, 0), (0, 352, 224, 0), (3, 352, 224, 0), (3, 0, 224, 0)],
+    3: [(3, 0, 128, 0), (3, 128, 128, 0), (0, 128, 128, 0), (3, 256, 160, 0), (0, 256, 160, 0), (3, 416, 160, 2),
+        (0, 416, 160, 2)],
     1: [(1, 0, 128, 0), (1, 128, 128, 0), (1, 256, 128, 0), (1, 384, 128, 0),
-        (4, 256, 128, 0), (4, 384, 128, 2), (4, 128, 128, 2), (4, 0, 128, 2)],
-    4: [(4, 96, 160, 0), (4, 256, 128, 0), (1, 256, 128, 0), (4, 384, 224, 0), (1, 384, 224, 2), (1, 96, 160, 2)],
-    2: [(2, 0, 128, 0), (2, 128, 160, 0), (2, 288, 224, 0), (5, 128, 160, 0), (5, 288, 224, 2), (5, 0, 128, 2)],
-    5: [(5, 0, 128, 0), (5, 128, 160, 0), (2, 128, 160, 0), (5, 288, 224, 0), (2, 288, 224, 2), (2, 0, 128, 2)],
+        (4, 128, 128, 0), (4, 256, 128, 2), (4, 384, 128, 2), (4, 0, 128, 2)],
+    4: [(4, 96, 128, 0), (4, 480, 128, 0), (1, 480, 128, 0), (4, 224, 128, 0), (1, 224, 128, 0), (4, 352, 128, 2),
+        (1, 352, 128, 2), (1, 96, 128, 0)],
+    2: [(2, 0, 128, 0), (2, 128, 128, 0), (5, 128, 128, 0), (2, 256, 128, 0), (5, 256, 128, 2), (2, 384, 128, 2),
+        (5, 384, 128, 2), (5, 0, 128, 0)],
+    5: [(5, 0, 128, 0), (5, 384, 128, 0), (2, 384, 128, 0), (5, 128, 128, 0), (2, 128, 128, 0), (5, 256, 128, 2),
+        (2, 256, 128, 2), (2, 0, 128, 0)],
 }
 XSEND = {
-    0: [[(0, 224, [4, 5], "all")]],
-    3: [[(0, 128, [4, 5], "lo"), (0, 128, [0], "hi")]],
-    1: [[(0, 160, [2], "lo"), (0, 160, [3], "hi")]],
-    4: [[(0, 224, [0, 2], "lo")], [(224, 256, [3, 5], "lo")], [(0, 96, [1], "hi")]],
-    2: [[(0, 128, [1], "lo"), (0, 128, [3], "hi")]],
-    5: [[(0, 128, [1, 3], "lo")]],
+    0: [[(0, 224, [5], "hi", "far"), (0, 224, [4], "lo", "near")]],
+    3: [[(0, 128, [4, 5], "lo", ""), (0, 128, [0], "hi", "")]],
+    1: [[(0, 160, [2], "lo", ""), (0, 160, [3], "hi", "far")]],
+    4: [[(0, 224, [0, 2], "lo", "")], [(224, 256, [3, 5], "lo", "")], [(0, 96, [1], "hi", "")]],
+    2: [[(0, 128, [3], "all", "far")], [(0, 128, [1], "lo", "")]],
+    5: [[(0, 128, [3, 1], "lo", "")]],
 }
-WENG = {0: "all", 1: "all", 2: "all", 3: "hi", 4: "hi", 5: "hi"}
-FIN = {0: [[5], [4]], 3: [[0], [4], [5]], 1: [[2], [3]], 4: [[2, 5], [0, 3]], 2: [[1], [3]], 5: [[1], [3]]}
-
+WENG = {0: "all", 1: "all", 2: "all", 3: "hi", 4: "all", 5: "all"}
+FIN = {
+    0: [(0, 96, 4, 0), (0, 96, 5, 1), (96, 224, 4, 0), (96, 224, 5, 1)],
+    3: [(0, 128, 0, 0), (0, 128, 5, 0), (0, 128, 4, 1)],
+    1: [(0, 160, 2, 0), (0, 160, 3, 1)],
+    4: [(0, 96, 2, 0), (96, 256, 2, 0), (0, 96, 0, 1), (96, 256, 0, 1)],
+    2: [(0, 128, 1, 0), (0, 128, 3, 1)],
+    5: [(0, 128, 3, 0), (0, 128, 1, 1)],
+}
+PARK = 640
 ZB, YB = 6, 2
 
 SCRATCH = {
     "xb": ("sbuf", [128, 1024], "bfloat16"),
     "wb": ("sbuf", [128, 2560], "bfloat16"),
-    "xq": ("sbuf", [128, 640], "float8_e4m3fn_x4"),
-    "xs": ("sbuf", [128, 640], "uint8"),
+    "xq": ("sbuf", [128, 896], "float8_e4m3fn_x4"),
+    "xs": ("sbuf", [128, 896], "uint8"),
     "wq": ("sbuf", [128, 640], "float8_e4m3fn_x4"),
     "ws": ("sbuf", [128, 640], "uint8"),
     "pq": ("sbuf", [128, 640], "float8_e4m3fn_x4"),
@@ -54,13 +65,51 @@ SCRATCH = {
     "yo": ("sbuf", [128, 256], "float32"),
     "ys": ("sbuf", [128, 512], "float32"),
 }
-SEMAPHORES = (["lx", "lwa", "lwb", "st", "qi", "mm", "ym", "zs", "zv", "hqd", "ev", "fa", "sent",
-               "wpa", "wpb", "hc", "hsc", "hr"]
-              + ["x%d" % i for i in range(6)] + ["r%d" % i for i in range(6)])
 
 
 def _bits(m):
     return bin(m).count("1")
+
+
+def _xsem(r, a):
+    return "x%d_%d" % (r, a)
+
+
+def _groups(r):
+    d = {}
+    for k, (w, s, n, lag) in enumerate(TILES[r]):
+        d.setdefault((s, n), []).append(k)
+    return sorted(d.items(), key=lambda e: e[1][-1])
+
+
+def _pieces(r, s, n):
+    out, p = [], 0
+    for (c, a, b) in LAY[r]:
+        lo, hi = max(s, p), min(s + n, p + b - a)
+        if lo < hi:
+            out.append((c, a + lo - p, a + hi - p, lo - s))
+        p += b - a
+    return out
+
+
+def _results(r):
+    out, y = [], 0
+    for gi, ((s, n), ks) in enumerate(_groups(r)):
+        for (c, a, b, at) in _pieces(r, s, n):
+            if c != r:
+                out.append((gi, c, a, b, y))
+                y += b - a
+    return out
+
+
+def _chunks(c, r):
+    return [t for call in XSEND[c] for t in call if r in t[2]]
+
+
+SEMAPHORES = (["lx", "lwa", "lwb", "st", "qi", "mm", "ym", "zs", "zv", "hqd", "ev", "fa", "sent",
+               "wpa", "wpb", "hc", "hsc", "hr"]
+              + sorted(set(_xsem(r, t[0]) for r in XSEND for call in XSEND[r] for t in call))
+              + sorted(set("r%d_%d" % (r, e[2]) for r in LAY for e in _results(r))))
 
 
 def _masks(topo, cores, core):
@@ -70,48 +119,30 @@ def _masks(topo, cores, core):
     return {"lo": lo, "all": al, "hi": al & ~lo}
 
 
-def _helpers(topo, cores):
-    out = {}
-    for r in range(len(cores)):
-        for c in range(len(cores)):
-            src, dst = cores[r], cores[c]
-            if topo.may_write(src, dst) or not _sends(r, c):
-                continue
-            ch = topo.chip(src)
-            first = src
-            while first > 0 and topo.chip(first - 1) == ch:
-                first -= 1
-            k = first
-            while topo.chip(k) == ch:
-                if k not in cores and k not in out.values() and topo.die(k) != topo.die(src) and topo.may_write(k, dst):
-                    out[(r, c)] = k
-                    break
-                k += 1
-    return out
+def _partner(topo, cores, r):
+    return [q for q in range(len(cores)) if q != r and topo.chip(cores[q]) == topo.chip(cores[r])][0]
 
 
-def _sends(r, c):
-    return any(c in t[2] for call in XSEND[r] for t in call)
-
-
-def _xpos(r, c):
-    p = 0
-    for (k, a, b) in LAY[r]:
-        if k == c:
-            return p, a, b
-        p += b - a
-    return None
+def _helper(topo, cores, r, dsts):
+    src = cores[r]
+    k = src
+    while k > 0 and topo.chip(k - 1) == topo.chip(src):
+        k -= 1
+    while topo.chip(k) == topo.chip(src):
+        if k not in cores and topo.die(k) != topo.die(src) and all(topo.may_write(k, cores[c]) for c in dsts):
+            return k
+        k += 1
+    raise ValueError("no helper")
 
 
 def rank_program(g, core, T, topo):
     cores = list(T.cores)
     rank = T.rank_of(core)
-    helpers = _helpers(topo, cores)
     chips = []
     for c in cores:
         if topo.chip(c) not in chips:
             chips.append(topo.chip(c))
-    if rank is None and core not in helpers.values():
+    if topo.chip(core) not in chips:
         return
     M = _masks(topo, cores, core)
     S = T.sem
@@ -142,36 +173,52 @@ def rank_program(g, core, T, topo):
     def codes(t, a, b):
         return t[:, a:b].bitcast(dt.uint8)
 
+    def xcol(r, c, a):
+        p = 0
+        for (k, ka, kb) in LAY[r]:
+            if k == c:
+                return p + a - ka
+            p += kb - ka
+
+    def layer(c):
+        return T["l%d" % chips.index(topo.chip(c))]
+
+    def pass_on(r, kind):
+        for call in XSEND[r]:
+            for (a, b, ds, e, via) in call:
+                if via == kind and (kind == "near" or _helper(topo, cores, r, ds) == core):
+                    n = b - a
+                    cols = [(c, xcol(c, r, a)) for c in ds]
+                    inc("hc", _bits(M[e])), inc("hsc", _bits(M[e]))
+                    wait("g", "hc", _bits(M[e]))
+                    send([(codes(T.xq, PARK, PARK + n), [(cores[c], codes(T.xq, p, p + n)) for c, p in cols], M["lo"],
+                           _xsem(r, a))])
+                    wait("g", "hsc", _bits(M[e]))
+                    send([(T.xs[:, PARK:PARK + n], [(cores[c], T.xs[:, p:p + n]) for c, p in cols], M["lo"],
+                           _xsem(r, a))])
+
     def finish():
         for name in total:
             if top.get(name, 0) < total[name]:
                 wait("g", name, total[name])
 
     if rank is None:
-        for (r, c), h in helpers.items():
-            if h != core:
+        for r in range(len(cores)):
+            if topo.chip(cores[r]) != topo.chip(core):
                 continue
-            n = [(a, b) for call in XSEND[r] for (a, b, ds, e) in call if c in ds][0]
-            e = [e for call in XSEND[r] for (a, b, ds, e) in call if c in ds][0]
-            n = n[1] - n[0]
-            p = _xpos(c, r)[0]
-            cnt = _bits(M[e])
-            wait("g", "hc", cnt)
-            send([(codes(T.xq, 0, n), [(cores[c], codes(T.xq, p, p + n))], M["lo"], "x%d" % r)])
-            wait("g", "hsc", cnt)
-            send([(T.xs[:, 0:n], [(cores[c], T.xs[:, p:p + n])], M["lo"], "x%d" % r)])
-            pos = _xpos(r, c)
-            if pos is not None:
-                _, a, b = pos
-                wait("g", "hr", _bits(M["all"]))
-                lay = T["l%d" % chips.index(topo.chip(core))]
-                send([(T.ys[:, 0:b - a], [(cores[c], lay[:, a:b])], M["lo"], "r%d" % r)])
+            pass_on(r, "far")
+            for (gi, c, a, b, y0) in _results(r):
+                if not topo.may_write(cores[r], cores[c]) and _helper(topo, cores, r, [c]) == core:
+                    wait("g", "hr", _bits(M["all"]))
+                    send([(T.ys[:, 0:b - a], [(cores[c], layer(core)[:, a:b])], M["lo"], "r%d_%d" % (r, a))])
         finish()
         return
 
     wid = T.tables["WID"][rank]
-    partner = [r for r in range(len(cores)) if r != rank and topo.chip(cores[r]) == topo.chip(core)][0]
-    on_chip = lambda c: topo.chip(cores[c]) == topo.chip(core)
+    partner = _partner(topo, cores, rank)
+
+    def on_chip(c):
+        return topo.chip(cores[c]) == topo.chip(core)
 
     g.sync.dma_start(T.xb[:, 0:4 * wid], T.x[:, 0:4 * wid]).then_inc(S.lx, 16)
     g.sync.dma_start(T.wb[:, 0:1024], T.w1[:, 0:1024]).then_inc(S.lwa, 16)
@@ -190,18 +237,17 @@ def rank_program(g, core, T, topo):
     wait("g", "qi", 1)
     for call in XSEND[rank]:
         cs, ss = [], []
-        for (a, b, ds, e) in call:
-            relay = [(rank, c) in helpers for c in ds]
-            dc, dp = [], []
-            for c in ds:
-                if (rank, c) in helpers:
-                    h, p = helpers[(rank, c)], 0
-                else:
-                    h, p = cores[c], _xpos(c, rank)[0]
-                dc.append((h, codes(T.xq, p, p + b - a)))
-                dp.append((h, T.xs[:, p:p + b - a]))
-            cs.append((codes(T.xq, a, b), dc, M[e], "hc" if relay[0] else "x%d" % rank))
-            ss.append((T.xs[:, a:b], dp, M[e], "hsc" if relay[0] else "x%d" % rank))
+        for (a, b, ds, e, via) in call:
+            if via == "near":
+                to = [(cores[partner], PARK)]
+            elif via == "far":
+                to = [(_helper(topo, cores, rank, ds), PARK)]
+            else:
+                to = [(cores[c], xcol(c, rank, a)) for c in ds]
+            cs.append((codes(T.xq, a, b), [(d, codes(T.xq, p, p + b - a)) for d, p in to], M[e],
+                       "hc" if via else _xsem(rank, a)))
+            ss.append((T.xs[:, a:b], [(d, T.xs[:, p:p + b - a]) for d, p in to], M[e],
+                       "hsc" if via else _xsem(rank, a)))
         send(cs)
         send(ss)
     pc = cores[partner]
@@ -209,40 +255,26 @@ def rank_program(g, core, T, topo):
         wait("g", "qi", q)
         send([(codes(T.wq, a, b), [(pc, codes(T.pq, a, b))], M[WENG[rank]], sem)])
         send([(T.ws[:, a:b], [(pc, T.ps[:, a:b])], M[WENG[rank]], sem)])
+    pass_on(partner, "near")
     wcnt = 2 * _bits(M[WENG[partner]])
     inc("wpa", wcnt), inc("wpb", wcnt)
     xcnt = 2 * _bits(M["lo"])
     for (c, a, b) in LAY[rank][1:]:
-        inc("x%d" % c, xcnt)
+        for t in _chunks(c, rank):
+            inc(_xsem(c, t[0]), xcnt)
 
     tiles = TILES[rank]
-    groups = {}
-    off = 0
-    toff = []
-    for k, (w, s, n, lag) in enumerate(tiles):
-        groups.setdefault((s, n), []).append(k)
-        toff.append(off)
-        off += n
-
-    mm = 0
-    drain = {}
-    ybank = {}
+    groups = _groups(rank)
+    toff = [sum(t[2] for t in tiles[:k]) for k in range(len(tiles))]
     evac_of = []
-    evcount = 0
-    yoff = 0
-    results = []
-    own_ev = 0
-    lagged = None
-    cs_, cv_ = 0, 0
+    own_ev = {}
+    yoff = [0]
 
-    def second(key):
-        gi = len(ybank)
-        ybank[key] = gi
-        ks = groups[key]
-        n = key[1]
+    def second(gi):
+        (s, n), ks = groups[gi]
         if gi >= YB:
             wait("t", "ev", evac_of[gi - YB])
-        out = T.yb[:, 512 * (gi % YB):512 * (gi % YB) + n]
+        base = 512 * (gi % YB)
         for i, k in enumerate(ks):
             own_w = tiles[k][0] == rank
             if own_w:
@@ -252,46 +284,31 @@ def rank_program(g, core, T, topo):
             wait("t", "hqd", k + 1)
             W, P = (T.wq, T.ws) if own_w else (T.pq, T.ps)
             o = toff[k]
-            ins = g.tensor.matmul_mx(out, W[:, 512:640], P[:, 512:640], T.hq[:, o:o + n], T.hs[:, o:o + n],
-                                     i == 0, i == len(ks) - 1)
-            if i == len(ks) - 1:
-                ins.then_inc(S.ym, 1)
-                inc("ym")
-
-    def evacuate(key, state):
-        s, n = key
-        gi = ybank[key]
+            ins = g.tensor.matmul_mx(T.yb[:, base:base + n], W[:, 512:640], P[:, 512:640], T.hq[:, o:o + n],
+                                     T.hs[:, o:o + n], i == 0, i == len(ks) - 1)
+        ins.then_inc(S.ym, 1)
+        inc("ym")
         wait("s", "ym", gi + 1)
-        base = 512 * (gi % YB)
-        p = 0
         runs = []
-        for (c, a, b) in LAY[rank]:
-            lo, hi = max(s, p), min(s + n, p + b - a)
-            if lo < hi:
-                piece = (c, a + lo - p, a + hi - p, lo - s)
-                kind = c == rank
-                if runs and runs[-1][0] == kind:
-                    runs[-1][1].append(piece)
-                else:
-                    runs.append((kind, [piece]))
-            p += b - a
-        for kind, pieces in runs:
-            lo, m = pieces[0][3], sum(q[2] - q[1] for q in pieces)
-            if kind:
-                out = T.own[:, pieces[0][1]:pieces[0][1] + m]
+        for piece in _pieces(rank, s, n):
+            if runs and (runs[-1][0][0] == rank) == (piece[0] == rank):
+                runs[-1].append(piece)
             else:
-                out = T.ys[:, state["y"]:state["y"] + m]
-            g.scalar.activation(out, T.yb[:, base + lo:base + lo + m], ActivationFunctionType.Copy).then_inc(S.ev, 1)
-            ev = inc("ev")
-            if kind:
-                state["own"] = ev
+                runs.append([piece])
+        for run in sorted(runs, key=lambda u: u[0][0] == rank):
+            at, m = run[0][3], sum(q[2] - q[1] for q in run)
+            if run[0][0] == rank:
+                out = T.own[:, run[0][1]:run[0][1] + m]
+                own_ev[(run[0][1], run[0][1] + m)] = total.get("ev", 0) + 1
             else:
-                for (c, a, b, at) in pieces:
-                    results.append((ev, state["y"] + at - lo, b - a, c, a))
-                state["y"] += m
+                out = T.ys[:, yoff[0]:yoff[0] + m]
+                yoff[0] += m
+            g.scalar.activation(out, T.yb[:, base + at:base + at + m], ActivationFunctionType.Copy).then_inc(S.ev, 1)
+            inc("ev")
         evac_of.append(total["ev"])
 
-    state = {"y": 0, "own": 0}
+    mm = 0
+    drain = []
     pending = None
     for k, (w, s, n, lag) in enumerate(tiles):
         own_w = w == rank
@@ -300,17 +317,15 @@ def rank_program(g, core, T, topo):
         for b in range(4):
             if pending is not None and b == lag:
                 second(pending)
-                evacuate(pending, state)
                 pending = None
             if b == 0:
-                p = 0
-                for (c, ca, cb) in LAY[rank]:
-                    if max(s, p) < min(s + n, p + cb - ca):
-                        if c == rank:
-                            wait("t", "qi", 1)
-                        else:
-                            wait("t", "x%d" % c, xcnt)
-                    p += cb - ca
+                for (c, ca, cb, at) in _pieces(rank, s, n):
+                    if c == rank:
+                        wait("t", "qi", 1)
+                    else:
+                        for t in _chunks(c, rank):
+                            if max(ca, t[0]) < min(cb, t[1]):
+                                wait("t", _xsem(c, t[0]), xcnt)
             if own_w:
                 wait("t", "qi", 2 if b < 2 else 3)
             else:
@@ -320,61 +335,59 @@ def rank_program(g, core, T, topo):
             z = T.z[:, 512 * (mm % ZB):512 * (mm % ZB) + n]
             g.tensor.matmul_mx(z, W[:, 128 * b:128 * b + 128], P[:, 128 * b:128 * b + 128],
                                T.xq[:, s:s + n], T.xs[:, s:s + n], True, True).then_inc(S.mm, 1)
-            inc("mm")
-            mm += 1
+            mm = inc("mm")
             h = T.hb[:, o + b:o + 4 * n:4]
             if b % 2 == 0:
                 wait("s", "mm", mm)
                 g.scalar.activation(h, z, ActivationFunctionType.Relu, scale=C).then_inc(S.zs, 1)
-                drain[mm - 1] = ("zs", inc("zs"))
+                drain.append(("zs", inc("zs")))
             else:
                 wait("v", "mm", mm)
                 g.vector.tensor_scalar(h, z, 0.0, C, AluOpType.max, AluOpType.mult).then_inc(S.zv, 1)
-                drain[mm - 1] = ("zv", inc("zv"))
+                drain.append(("zv", inc("zv")))
         wait("v", "zs", total["zs"])
         wait("v", "zv", total["zv"])
         g.vector.quantize_mx(T.hq[:, toff[k]:toff[k] + n], T.hs[:, toff[k]:toff[k] + n],
                              T.hb[:, o:o + 4 * n]).then_inc(S.hqd, 1)
         inc("hqd")
-        if groups[(s, n)][-1] == k:
-            pending = (s, n)
+        for gi, (key, ks) in enumerate(groups):
+            if ks[-1] == k:
+                pending = gi
     second(pending)
-    evacuate(pending, state)
 
-    for (ev, y0, n, c, a) in results:
-        wait("g", "ev", ev)
-        src = T.ys[:, y0:y0 + n]
-        if (rank, c) in helpers:
-            send([(src, [(helpers[(rank, c)], T.ys[:, 0:n])], M["all"], "hr")])
+    for (gi, c, a, b, y0) in _results(rank):
+        wait("g", "ev", evac_of[gi])
+        src, sem = T.ys[:, y0:y0 + b - a], "r%d_%d" % (rank, a)
+        if not topo.may_write(core, cores[c]):
+            send([(src, [(_helper(topo, cores, rank, [c]), T.ys[:, 0:b - a])], M["all"], "hr")])
             continue
-        if on_chip(c) and (len([1 for t in TILES[c] if t[1] <= a < t[1] + t[2]]) == 0):
-            dst, m = T.own[:, a:a + n], M["all"]
-        else:
-            dst, m = T["l%d" % chips.index(topo.chip(core))][:, a:a + n], M["all"] if on_chip(c) else M["lo"]
-        send([(src, [(cores[c], dst)], m, "r%d" % rank)])
+        mine = any(q[0] == c and q[1] <= a < q[2] for t in TILES[c] for q in _pieces(c, t[1], t[2]))
+        dst = T.own if on_chip(c) and not mine else layer(core)
+        send([(src, [(cores[c], dst[:, a:b])], M["all" if on_chip(c) else "lo"], sem)])
 
-    rcnt = {}
+    arrive = []
     for r in range(len(cores)):
-        if r != rank and _xpos(r, rank) is not None:
-            rcnt[r] = _bits(M["all"] if on_chip(r) else M["lo"])
-            inc("r%d" % r, rcnt[r])
-    wait("v", "ev", state["own"])
-    layers = FIN[rank]
-    for r in rcnt:
-        if on_chip(r) and [r] not in layers:
-            wait("v", "r%d" % r, rcnt[r])
-    acc = T.own
-    for i, senders in enumerate(layers):
-        for r in senders:
-            wait("v", "r%d" % r, rcnt[r])
-        if i:
-            wait("v", "fa", i)
-        lay = T["l%d" % chips.index(topo.chip(cores[senders[0]]))]
-        g.vector.tensor_tensor(T.yo[:, 0:wid], acc[:, 0:wid], lay[:, 0:wid], AluOpType.add).then_inc(S.fa, 1)
-        inc("fa")
-        acc = T.yo
-    wait("y", "fa", len(layers))
-    g.sync.dma_start(T.y[:, 0:wid], T.yo[:, 0:wid]).then_inc(S.st, 16)
-    inc("st", 16)
-    wait("y", "st", 16)
+        if r != rank:
+            for (gi, c, a, b, y0) in _results(r):
+                if c == rank:
+                    arrive.append((r, a, b, "r%d_%d" % (r, a), _bits(M["all" if on_chip(r) else "lo"])))
+                    inc(arrive[-1][3], arrive[-1][4])
+    done = {}
+    for (a, b, l, last) in FIN[rank]:
+        for (oa, ob) in own_ev:
+            if max(oa, a) < min(ob, b):
+                wait("v", "ev", own_ev[(oa, ob)])
+        for (r, ra, rb, sem, cnt) in arrive:
+            if max(ra, a) < min(rb, b) and (on_chip(r) or topo.chip(cores[r]) == topo.chip(cores[l])):
+                wait("v", sem, cnt)
+        if (a, b) in done:
+            wait("v", "fa", done[(a, b)])
+        acc = T.yo if (a, b) in done else T.own
+        g.vector.tensor_tensor(T.yo[:, a:b], acc[:, a:b], layer(cores[l])[:, a:b], AluOpType.add).then_inc(S.fa, 1)
+        done[(a, b)] = inc("fa")
+        if last:
+            wait("y", "fa", done[(a, b)])
+            g.sync.dma_start(T.y[:, a:b], T.yo[:, a:b]).then_inc(S.st, 16)
+            inc("st", 16)
+    wait("y", "st", total["st"])
     finish()

import numpy as np
from concourse.bass import DstId, RemoteDMATransfer
from concourse.mybir import dt, AluOpType, ActivationFunctionType

C = float(np.float32(0.043))
LAY = {
    0: [(0, 0, 224), (3, 0, 128), (4, 0, 224)],
    3: [(3, 0, 128), (5, 0, 128), (4, 224, 256), (2, 0, 128), (1, 0, 160)],
    1: [(1, 0, 160), (4, 0, 96), (2, 0, 128), (5, 0, 128)],
    4: [(4, 0, 256), (0, 0, 224), (3, 0, 128)],
    2: [(2, 0, 128), (1, 0, 160), (4, 0, 224)],
    5: [(5, 0, 128), (4, 224, 256), (0, 0, 224), (3, 0, 128)],
}
TILES = {
    0: [(0, 0, 224, 0), (0, 224, 128, 0), (0, 352, 224, 0), (3, 352, 224, 0), (3, 0, 224, 0)],
    3: [(3, 0, 128, 0), (3, 128, 128, 0), (0, 128, 128, 0), (3, 256, 160, 0), (0, 256, 160, 0), (3, 416, 160, 2),
        (0, 416, 160, 2)],
    1: [(1, 0, 128, 0), (1, 128, 128, 0), (1, 256, 128, 0), (1, 384, 128, 0),
        (4, 128, 128, 0), (4, 256, 128, 2), (4, 384, 128, 2), (4, 0, 128, 2)],
    4: [(4, 96, 128, 0), (4, 480, 128, 0), (1, 480, 128, 0), (4, 224, 128, 0), (1, 224, 128, 0), (4, 352, 128, 2),
        (1, 352, 128, 2), (1, 96, 128, 0)],
    2: [(2, 0, 128, 0), (2, 128, 128, 0), (5, 128, 128, 0), (2, 256, 128, 0), (5, 256, 128, 2), (2, 384, 128, 2),
        (5, 384, 128, 2), (5, 0, 128, 0)],
    5: [(5, 0, 128, 0), (5, 384, 128, 0), (2, 384, 128, 0), (5, 128, 128, 0), (2, 128, 128, 0), (5, 256, 128, 2),
        (2, 256, 128, 2), (2, 0, 128, 0)],
}
XSEND = {
    0: [[(0, 224, [5], "hi", "far"), (0, 224, [4], "lo", "near")]],
    3: [[(0, 128, [4, 5], "lo", ""), (0, 128, [0], "hi", "")]],
    1: [[(0, 160, [2], "lo", ""), (0, 160, [3], "hi", "far")]],
    4: [[(0, 224, [0, 2], "lo", "")], [(224, 256, [3, 5], "lo", "")], [(0, 96, [1], "hi", "")]],
    2: [[(0, 128, [3], "all", "far")], [(0, 128, [1], "lo", "")]],
    5: [[(0, 128, [3, 1], "lo", "")]],
}
WENG = {0: "all", 1: "all", 2: "all", 3: "hi", 4: "all", 5: "all"}
FIN = {
    0: [(0, 96, 4, 0), (0, 96, 5, 1), (96, 224, 4, 0), (96, 224, 5, 1)],
    3: [(0, 128, 0, 0), (0, 128, 5, 0), (0, 128, 4, 1)],
    1: [(0, 160, 2, 0), (0, 160, 3, 1)],
    4: [(0, 96, 2, 0), (96, 256, 2, 0), (0, 96, 0, 1), (96, 256, 0, 1)],
    2: [(0, 128, 1, 0), (0, 128, 3, 1)],
    5: [(0, 128, 3, 0), (0, 128, 1, 1)],
}
PARK = 640
ZB, YB = 6, 2

SCRATCH = {
    "xb": ("sbuf", [128, 1024], "bfloat16"),
    "wb": ("sbuf", [128, 2560], "bfloat16"),
    "xq": ("sbuf", [128, 896], "float8_e4m3fn_x4"),
    "xs": ("sbuf", [128, 896], "uint8"),
    "wq": ("sbuf", [128, 640], "float8_e4m3fn_x4"),
    "ws": ("sbuf", [128, 640], "uint8"),
    "pq": ("sbuf", [128, 640], "float8_e4m3fn_x4"),
    "ps": ("sbuf", [128, 640], "uint8"),
    "hb": ("sbuf", [128, 4096], "bfloat16"),
    "hq": ("sbuf", [128, 1024], "float8_e4m3fn_x4"),
    "hs": ("sbuf", [128, 1024], "uint8"),
    "z": ("psum", [128, 512 * ZB], "float32"),
    "yb": ("psum", [128, 512 * YB], "float32"),
    "own": ("sbuf", [128, 256], "float32"),
    "l0": ("sbuf", [128, 256], "float32"),
    "l1": ("sbuf", [128, 256], "float32"),
    "l2": ("sbuf", [128, 256], "float32"),
    "yo": ("sbuf", [128, 256], "float32"),
    "ys": ("sbuf", [128, 512], "float32"),
}


def _bits(m):
    return bin(m).count("1")


def _xsem(r, a):
    return "x%d_%d" % (r, a)


def _groups(r):
    d = {}
    for k, (w, s, n, lag) in enumerate(TILES[r]):
        d.setdefault((s, n), []).append(k)
    return sorted(d.items(), key=lambda e: e[1][-1])


def _pieces(r, s, n):
    out, p = [], 0
    for (c, a, b) in LAY[r]:
        lo, hi = max(s, p), min(s + n, p + b - a)
        if lo < hi:
            out.append((c, a + lo - p, a + hi - p, lo - s))
        p += b - a
    return out


def _results(r):
    out, y = [], 0
    for gi, ((s, n), ks) in enumerate(_groups(r)):
        for (c, a, b, at) in _pieces(r, s, n):
            if c != r:
                out.append((gi, c, a, b, y))
                y += b - a
    return out


def _chunks(c, r):
    return [t for call in XSEND[c] for t in call if r in t[2]]


SEMAPHORES = (["lx", "lwa", "lwb", "st", "qi", "mm", "ym", "zs", "zv", "hqd", "ev", "fa", "sent",
               "wpa", "wpb", "hc", "hsc", "hr"]
              + sorted(set(_xsem(r, t[0]) for r in XSEND for call in XSEND[r] for t in call))
              + sorted(set("r%d_%d" % (r, e[2]) for r in LAY for e in _results(r))))


def _masks(topo, cores, core):
    far = [c for c in cores if topo.chip(c) != topo.chip(core)][0]
    near = [c for c in cores if topo.chip(c) == topo.chip(core) and c != core][0]
    lo, al = topo.mask(core, far), topo.mask(core, near)
    return {"lo": lo, "all": al, "hi": al & ~lo}


def _partner(topo, cores, r):
    return [q for q in range(len(cores)) if q != r and topo.chip(cores[q]) == topo.chip(cores[r])][0]


def _helper(topo, cores, r, dsts):
    src = cores[r]
    k = src
    while k > 0 and topo.chip(k - 1) == topo.chip(src):
        k -= 1
    while topo.chip(k) == topo.chip(src):
        if k not in cores and topo.die(k) != topo.die(src) and all(topo.may_write(k, cores[c]) for c in dsts):
            return k
        k += 1
    raise ValueError("no helper")


def rank_program(g, core, T, topo):
    cores = list(T.cores)
    rank = T.rank_of(core)
    chips = []
    for c in cores:
        if topo.chip(c) not in chips:
            chips.append(topo.chip(c))
    if topo.chip(core) not in chips:
        return
    M = _masks(topo, cores, core)
    S = T.sem
    seen, top, total = {}, {}, {}
    Q = {"g": g, "t": g.tensor, "v": g.vector, "s": g.scalar, "y": g.sync}

    def wait(q, name, val):
        if seen.get((q, name), 0) < val:
            Q[q].wait_ge(S[name], val)
            seen[(q, name)] = val
            top[name] = max(top.get(name, 0), val)

    def inc(name, n=1):
        total[name] = total.get(name, 0) + n
        return total[name]

    def did(dst):
        rid, pid, _ = topo.addr(dst)
        return DstId(rid=rid, pnc=pid)

    def send(transfers):
        g.remote_dma_fused([RemoteDMATransfer(dst_ids=[did(d) for d, _ in ds], dma_engine_mask=m, remote_sem=S[sem],
                                              srcs=[src], dsts=[ap for _, ap in ds], alu_op=0)
                            for (src, ds, m, sem) in transfers], local_sem=S.sent)
        for (src, ds, m, sem) in transfers:
            inc("sent", _bits(m))

    def codes(t, a, b):
        return t[:, a:b].bitcast(dt.uint8)

    def xcol(r, c, a):
        p = 0
        for (k, ka, kb) in LAY[r]:
            if k == c:
                return p + a - ka
            p += kb - ka

    def layer(c):
        return T["l%d" % chips.index(topo.chip(c))]

    def pass_on(r, kind):
        for call in XSEND[r]:
            for (a, b, ds, e, via) in call:
                if via == kind and (kind == "near" or _helper(topo, cores, r, ds) == core):
                    n = b - a
                    cols = [(c, xcol(c, r, a)) for c in ds]
                    inc("hc", _bits(M[e])), inc("hsc", _bits(M[e]))
                    wait("g", "hc", _bits(M[e]))
                    send([(codes(T.xq, PARK, PARK + n), [(cores[c], codes(T.xq, p, p + n)) for c, p in cols], M["lo"],
                           _xsem(r, a))])
                    wait("g", "hsc", _bits(M[e]))
                    send([(T.xs[:, PARK:PARK + n], [(cores[c], T.xs[:, p:p + n]) for c, p in cols], M["lo"],
                           _xsem(r, a))])

    def finish():
        for name in total:
            if top.get(name, 0) < total[name]:
                wait("g", name, total[name])

    if rank is None:
        for r in range(len(cores)):
            if topo.chip(cores[r]) != topo.chip(core):
                continue
            pass_on(r, "far")
            for (gi, c, a, b, y0) in _results(r):
                if not topo.may_write(cores[r], cores[c]) and _helper(topo, cores, r, [c]) == core:
                    wait("g", "hr", _bits(M["all"]))
                    send([(T.ys[:, 0:b - a], [(cores[c], layer(core)[:, a:b])], M["lo"], "r%d_%d" % (r, a))])
        finish()
        return

    wid = T.tables["WID"][rank]
    partner = _partner(topo, cores, rank)

    def on_chip(c):
        return topo.chip(cores[c]) == topo.chip(core)

    g.sync.dma_start(T.xb[:, 0:4 * wid], T.x[:, 0:4 * wid]).then_inc(S.lx, 16)
    g.sync.dma_start(T.wb[:, 0:1024], T.w1[:, 0:1024]).then_inc(S.lwa, 16)
    g.sync.dma_start(T.wb[:, 1024:2048], T.w1[:, 1024:2048]).then_inc(S.lwb, 16)
    g.sync.dma_start(T.wb[:, 2048:2560], T.w2[:]).then_inc(S.lwb, 16)
    inc("lx", 16), inc("lwa", 16), inc("lwb", 32)
    wait("v", "lx", 16)
    g.vector.quantize_mx(T.xq[:, 0:wid], T.xs[:, 0:wid], T.xb[:, 0:4 * wid]).then_inc(S.qi, 1)
    wait("v", "lwa", 16)
    g.vector.quantize_mx(T.wq[:, 0:256], T.ws[:, 0:256], T.wb[:, 0:1024]).then_inc(S.qi, 1)
    wait("v", "lwb", 32)
    g.vector.quantize_mx(T.wq[:, 256:512], T.ws[:, 256:512], T.wb[:, 1024:2048]).then_inc(S.qi, 1)
    g.vector.quantize_mx(T.wq[:, 512:640], T.ws[:, 512:640], T.wb[:, 2048:2560]).then_inc(S.qi, 1)
    inc("qi", 4)

    wait("g", "qi", 1)
    for call in XSEND[rank]:
        cs, ss = [], []
        for (a, b, ds, e, via) in call:
            if via == "near":
                to = [(cores[partner], PARK)]
            elif via == "far":
                to = [(_helper(topo, cores, rank, ds), PARK)]
            else:
                to = [(cores[c], xcol(c, rank, a)) for c in ds]
            cs.append((codes(T.xq, a, b), [(d, codes(T.xq, p, p + b - a)) for d, p in to], M[e],
                       "hc" if via else _xsem(rank, a)))
            ss.append((T.xs[:, a:b], [(d, T.xs[:, p:p + b - a]) for d, p in to], M[e],
                       "hsc" if via else _xsem(rank, a)))
        send(cs)
        send(ss)
    pc = cores[partner]
    for (a, b, q, sem) in ((0, 256, 2, "wpa"), (256, 640, 4, "wpb")):
        wait("g", "qi", q)
        send([(codes(T.wq, a, b), [(pc, codes(T.pq, a, b))], M[WENG[rank]], sem)])
        send([(T.ws[:, a:b], [(pc, T.ps[:, a:b])], M[WENG[rank]], sem)])
    pass_on(partner, "near")
    wcnt = 2 * _bits(M[WENG[partner]])
    inc("wpa", wcnt), inc("wpb", wcnt)
    xcnt = 2 * _bits(M["lo"])
    for (c, a, b) in LAY[rank][1:]:
        for t in _chunks(c, rank):
            inc(_xsem(c, t[0]), xcnt)

    tiles = TILES[rank]
    groups = _groups(rank)
    toff = [sum(t[2] for t in tiles[:k]) for k in range(len(tiles))]
    evac_of = []
    own_ev = {}
    yoff = [0]

    def second(gi):
        (s, n), ks = groups[gi]
        if gi >= YB:
            wait("t", "ev", evac_of[gi - YB])
        base = 512 * (gi % YB)
        for i, k in enumerate(ks):
            own_w = tiles[k][0] == rank
            if own_w:
                wait("t", "qi", 4)
            else:
                wait("t", "wpb", wcnt)
            wait("t", "hqd", k + 1)
            W, P = (T.wq, T.ws) if own_w else (T.pq, T.ps)
            o = toff[k]
            ins = g.tensor.matmul_mx(T.yb[:, base:base + n], W[:, 512:640], P[:, 512:640], T.hq[:, o:o + n],
                                     T.hs[:, o:o + n], i == 0, i == len(ks) - 1)
        ins.then_inc(S.ym, 1)
        inc("ym")
        wait("s", "ym", gi + 1)
        runs = []
        for piece in _pieces(rank, s, n):
            if runs and (runs[-1][0][0] == rank) == (piece[0] == rank):
                runs[-1].append(piece)
            else:
                runs.append([piece])
        for run in sorted(runs, key=lambda u: u[0][0] == rank):
            at, m = run[0][3], sum(q[2] - q[1] for q in run)
            if run[0][0] == rank:
                out = T.own[:, run[0][1]:run[0][1] + m]
                own_ev[(run[0][1], run[0][1] + m)] = total.get("ev", 0) + 1
            else:
                out = T.ys[:, yoff[0]:yoff[0] + m]
                yoff[0] += m
            g.scalar.activation(out, T.yb[:, base + at:base + at + m], ActivationFunctionType.Copy).then_inc(S.ev, 1)
            inc("ev")
        evac_of.append(total["ev"])

    mm = 0
    drain = []
    pending = None
    for k, (w, s, n, lag) in enumerate(tiles):
        own_w = w == rank
        W, P = (T.wq, T.ws) if own_w else (T.pq, T.ps)
        o = 4 * toff[k]
        for b in range(4):
            if pending is not None and b == lag:
                second(pending)
                pending = None
            if b == 0:
                for (c, ca, cb, at) in _pieces(rank, s, n):
                    if c == rank:
                        wait("t", "qi", 1)
                    else:
                        for t in _chunks(c, rank):
                            if max(ca, t[0]) < min(cb, t[1]):
                                wait("t", _xsem(c, t[0]), xcnt)
            if own_w:
                wait("t", "qi", 2 if b < 2 else 3)
            else:
                wait("t", "wpa" if b < 2 else "wpb", wcnt)
            if mm >= ZB:
                wait("t", *drain[mm - ZB])
            z = T.z[:, 512 * (mm % ZB):512 * (mm % ZB) + n]
            g.tensor.matmul_mx(z, W[:, 128 * b:128 * b + 128], P[:, 128 * b:128 * b + 128],
                               T.xq[:, s:s + n], T.xs[:, s:s + n], True, True).then_inc(S.mm, 1)
            mm = inc("mm")
            h = T.hb[:, o + b:o + 4 * n:4]
            if b % 2 == 0:
                wait("s", "mm", mm)
                g.scalar.activation(h, z, ActivationFunctionType.Relu, scale=C).then_inc(S.zs, 1)
                drain.append(("zs", inc("zs")))
            else:
                wait("v", "mm", mm)
                g.vector.tensor_scalar(h, z, 0.0, C, AluOpType.max, AluOpType.mult).then_inc(S.zv, 1)
                drain.append(("zv", inc("zv")))
        wait("v", "zs", total["zs"])
        wait("v", "zv", total["zv"])
        g.vector.quantize_mx(T.hq[:, toff[k]:toff[k] + n], T.hs[:, toff[k]:toff[k] + n],
                             T.hb[:, o:o + 4 * n]).then_inc(S.hqd, 1)
        inc("hqd")
        for gi, (key, ks) in enumerate(groups):
            if ks[-1] == k:
                pending = gi
    second(pending)

    for (gi, c, a, b, y0) in _results(rank):
        wait("g", "ev", evac_of[gi])
        src, sem = T.ys[:, y0:y0 + b - a], "r%d_%d" % (rank, a)
        if not topo.may_write(core, cores[c]):
            send([(src, [(_helper(topo, cores, rank, [c]), T.ys[:, 0:b - a])], M["all"], "hr")])
            continue
        mine = any(q[0] == c and q[1] <= a < q[2] for t in TILES[c] for q in _pieces(c, t[1], t[2]))
        dst = T.own if on_chip(c) and not mine else layer(core)
        send([(src, [(cores[c], dst[:, a:b])], M["all" if on_chip(c) else "lo"], sem)])

    arrive = []
    for r in range(len(cores)):
        if r != rank:
            for (gi, c, a, b, y0) in _results(r):
                if c == rank:
                    arrive.append((r, a, b, "r%d_%d" % (r, a), _bits(M["all" if on_chip(r) else "lo"])))
                    inc(arrive[-1][3], arrive[-1][4])
    done = {}
    for (a, b, l, last) in FIN[rank]:
        for (oa, ob) in own_ev:
            if max(oa, a) < min(ob, b):
                wait("v", "ev", own_ev[(oa, ob)])
        for (r, ra, rb, sem, cnt) in arrive:
            if max(ra, a) < min(rb, b) and (on_chip(r) or topo.chip(cores[r]) == topo.chip(cores[l])):
                wait("v", sem, cnt)
        if (a, b) in done:
            wait("v", "fa", done[(a, b)])
        acc = T.yo if (a, b) in done else T.own
        g.vector.tensor_tensor(T.yo[:, a:b], acc[:, a:b], layer(cores[l])[:, a:b], AluOpType.add).then_inc(S.fa, 1)
        done[(a, b)] = inc("fa")
        if last:
            wait("y", "fa", done[(a, b)])
            g.sync.dma_start(T.y[:, a:b], T.yo[:, a:b]).then_inc(S.st, 16)
            inc("st", 16)
    wait("y", "st", total["st"])
    finish()
